import numpy as np
import ml_dtypes


def mxq(x, axis, fmt="e4m3"):
    dtype, down = {"e4m3": (ml_dtypes.float8_e4m3fn, 7), "e5m2": (ml_dtypes.float8_e5m2, 14)}[fmt]
    v = np.moveaxis(np.asarray(x, np.float32).astype(ml_dtypes.bfloat16).astype(np.float64), axis, -1)
    blocks = v.reshape(v.shape[:-1] + (-1, 32))
    amax = np.abs(blocks).max(-1, keepdims=True)
    byte = np.maximum(np.where(amax > 0, np.frexp(amax)[1] - 1 + 127, 0) - down, 1)
    scale = np.exp2(byte - 127.0)
    codes = (blocks / scale).astype(np.float32).astype(dtype).astype(np.float64)
    return np.moveaxis((codes * scale).reshape(v.shape), -1, axis)


WIDE = False


def mx_kscale(k):
    if not WIDE:
        return np.ones(k)
    levels = np.array([10, -10, 5, -5, 0])
    if k % 512:
        return np.exp2(np.random.permutation(np.resize(levels, k // 32))).repeat(32)
    a = np.empty((k // 512, 16))
    for p in range(k // 512):
        a[p, :8] = np.random.permutation(np.resize(levels, 8))
        for g in range(8):
            far = levels[np.abs(levels - a[p, g]) >= 10]
            a[p, g + 8] = far[np.random.randint(len(far))]
    return np.exp2(a.ravel()).repeat(32)


def f64(x):
    return np.asarray(x).astype(np.float64)


def striped(idx):
    return np.tile(np.asarray(idx).reshape(-1, 16).T, (8, 1)).astype(np.uint16)


def unstriped(offs):
    return offs[:16].T.reshape(-1).astype(np.int64)


E2M1 = np.array([0.0, 0.5, 1.0, 1.5, 2.0, 3.0, 4.0, 6.0, -0.0, -0.5, -1.0, -1.5, -2.0, -3.0, -4.0, -6.0])


def pack_weight(w, fmt):
    k, n = w.shape
    w = f64(np.asarray(w, np.float32).astype(ml_dtypes.bfloat16)).reshape(k // 32, 32, n)
    amax = np.abs(w).max(1)
    if fmt == "e4m3":
        byte = np.frexp(amax)[1] - 1 + 127 - 7
    else:
        mant, ex = np.frexp(amax / 6.0)
        byte = np.where(mant > 0.5, ex, ex - 1) + 127
    byte = np.clip(np.where(amax > 0, byte, 1), 1, 254)
    scaled = (w * np.exp2(127.0 - byte)[:, None, :]).reshape(k, n).astype(np.float32)
    by_word = np.ascontiguousarray(scaled.reshape(k // 512, 128, 4, n).transpose(0, 1, 3, 2))
    if fmt == "e4m3":
        words = by_word.astype(ml_dtypes.float8_e4m3fn).view(np.uint8)
    else:
        c = by_word.astype(ml_dtypes.float4_e2m1fn).view(np.uint8) & 0xF
        words = (c[..., 0::2] | (c[..., 1::2] << 4)).reshape(k // 512, 128, 2 * n)
    return np.ascontiguousarray(words), np.ascontiguousarray(byte.astype(np.uint8).reshape(k // 512, 16, n))


def unpack_weight(words, scales, fmt):
    g, _, n = scales.shape
    words = np.ascontiguousarray(words).reshape(g, 128, n, -1)
    if fmt == "e4m3":
        vals = words.view(ml_dtypes.float8_e4m3fn).astype(np.float64)
    else:
        nib = np.empty((g, 128, n, 4), np.uint8)
        nib[..., 0::2] = words & 0xF
        nib[..., 1::2] = words >> 4
        vals = E2M1[nib]
    vals = vals * np.repeat(np.exp2(scales.astype(np.float64) - 127.0), 8, axis=1)[..., None]
    return vals.transpose(0, 1, 3, 2).reshape(g * 512, n)


def bf(x):
    return np.asarray(x, np.float32).astype(ml_dtypes.bfloat16)


def planes(Y):
    r, m = Y.shape
    b = f64(bf(Y)).reshape(r // 32, 32, m)
    amax = np.abs(b).max(1)
    byte = np.clip(np.where(amax > 0, np.frexp(amax)[1] - 1 + 127 - 7, 1), 1, 254)
    codes = (b * np.exp2(127.0 - byte)[:, None, :]).reshape(r, m).astype(np.float32).astype(ml_dtypes.float8_e4m3fn).view(np.uint8)
    words = codes.reshape(r // 512, 128, 4, m).transpose(0, 1, 3, 2)
    return np.ascontiguousarray(words), np.ascontiguousarray(byte.astype(np.uint8).reshape(r // 512, 16, m))


D, T, I, Q, E, U, X = 512, 2048, 512, 256, 512, 1024, 1024


def setup_inputs():
    n = np.random.standard_normal
    idx = np.random.permutation(T)[:I]
    idx2 = np.random.permutation(U)[:Q]
    idx3 = np.random.permutation(X)[:I]
    fd = mx_kscale(D)
    fi = mx_kscale(I)
    keysp = pack_weight(n((D, T)) / fd[:, None], "e2m1")
    return {
        "users": (n((D, U)) * 1.0 / np.sqrt(D) * fd[:, None]).astype(np.float32),
        "keys_words": keysp[0],
        "keys_scales": keysp[1],
        "os": (np.random.uniform(0.02, 0.08, (1, I)) * fi).astype(np.float32),
        "vals": (n((E, T))).astype(np.float32),
        "vals2": (n((E, X))).astype(np.float32),
        "vsc": (np.random.uniform(0.5, 2.0, (1, I)) / fi).astype(np.float32),
        "offs": striped(idx),
        "offs2": striped(idx2),
        "offs3": striped(idx3),
    }


def reference(users, keys_words, keys_scales, os, vals, vals2, vsc, offs, offs2, offs3):
    idx = unstriped(offs)
    idx2 = unstriped(offs2)
    idx3 = unstriped(offs3)
    keysu = unpack_weight(keys_words, keys_scales, "e2m1")
    usersidx2q = mxq(f64(users)[:, idx2], 0, "e4m3")
    keysidxg = keysu[:, idx]
    w = usersidx2q.T @ keysidxg
    wo1 = w * f64(os)
    wt1 = wo1.T
    vz = np.maximum(f64(vals)[:, idx], f64(vals2)[:, idx3]) * f64(vsc)
    vt1 = vz.T
    vt1q = mxq(vt1, 0, "e4m3")
    wt1q = mxq(wt1, 0, "e4m3")
    o = vt1q.T @ wt1q
    words, scales = planes(o)
    return o, words, scales

@@ -1,0 +1,211 @@
+from contextlib import ExitStack
+
+import concourse.mybir as mybir
+from concourse.masks import make_identity
+
+D, T, I, Q, E, U, X = 512, 2048, 512, 256, 512, 1024, 1024
+FLOPS = 2 * D * I * Q + 2 * I * E * Q
+
+F32 = mybir.dt.float32
+BF16 = mybir.dt.bfloat16
+I32 = mybir.dt.int32
+U32 = mybir.dt.uint32
+U16 = mybir.dt.uint16
+U8 = mybir.dt.uint8
+FP8X4 = mybir.dt.float8_e4m3fn_x4
+FP4X4 = mybir.dt.float4_e2m1fn_x4
+COPY = mybir.ActivationFunctionType.Copy
+MULT = mybir.AluOpType.mult
+MAX = mybir.AluOpType.max
+
+P = 128
+PACK = 4
+RUN = 8
+HALF = Q // 2
+PER_COLUMN = 16
+SPLIT = 256
+
+
+def listed(view):
+    return view.rearrange("p (b t j) -> p b t j", t=PACK, j=RUN)
+
+
+def dealt(view):
+    return view.rearrange("p (t b j) -> p b t j", t=PACK, j=RUN)
+
+
+def tile_attend_listedqueries_mergedvalues_lean_pl_kernel(
+    tc, users, keys_words, keys_scales, weight_factor, vals, vals2, value_factor,
+    offs, offs2, offs3, out_0, out_1, out_2,
+):
+    nc = tc.nc
+    with ExitStack() as ctx:
+        held = ctx.enter_context(tc.tile_pool(name="held", bufs=1))
+        ring = ctx.enter_context(tc.tile_pool(name="ring", bufs=2))
+        psum = ctx.enter_context(tc.psum_pool(name="psum", bufs=1))
+
+        key_list = held.tile([P, I // PER_COLUMN], U16, name="key_list")
+        user_list = held.tile([P, Q // PER_COLUMN], U16, name="user_list")
+        second_list = held.tile([P, I // PER_COLUMN], U16, name="second_list")
+        key_words = held.tile([P, T], U16, name="key_words")
+        key_bytes = held.tile([P, T], U8, name="key_bytes")
+        factor_rows = held.tile([P, P], F32, name="factor_rows")
+        identity = held.tile([P, P], F32, name="identity")
+        user_rows = [held.tile([P, U], F32, name=f"user_rows{t}") for t in range(PACK)]
+        first_rows = [held.tile([P, T], F32, name=f"first_rows{t}") for t in range(PACK)]
+        second_rows = [held.tile([P, X], F32, name=f"second_rows{t}") for t in range(PACK)]
+
+        nc.vector.memset(key_bytes[:].bitcast(I32), 0)
+        nc.vector.memset(factor_rows[:], 0.0)
+        make_identity(nc, identity[:])
+
+        users_v = users.rearrange("(p t) u -> p t u", t=PACK)
+        vals_v = vals.rearrange("(p t) c -> p t c", t=PACK)
+        vals2_v = vals2.rearrange("(p t) c -> p t c", t=PACK)
+        out_v = out_0.rearrange("(p t) q -> p t q", t=PACK)
+
+        nc.sync.dma_start(key_words[:].bitcast(I32), keys_words[0].bitcast(I32))
+        nc.sync.dma_start(user_rows[0][:], users_v[:, 0, :])
+        nc.sync.dma_start(key_list[:], offs)
+        nc.sync.dma_start(user_list[:], offs2)
+        for quad in range(4):
+            nc.scalar.dma_start(
+                key_bytes[32 * quad : 32 * quad + 4, :].bitcast(I32),
+                keys_scales[0, 4 * quad : 4 * quad + 4, :].bitcast(I32),
+            )
+        for place, factor in enumerate((weight_factor, value_factor)):
+            nc.scalar.dma_start(
+                factor_rows[PACK * place : PACK * place + PACK, :].rearrange("t (b j) -> t b j", j=RUN),
+                factor[0].rearrange("(b t j) -> t b j", t=PACK, j=RUN),
+            )
+        for t in range(1, PACK):
+            nc.sync.dma_start(user_rows[t][:], users_v[:, t, :])
+        nc.sync.dma_start(second_list[:], offs3)
+        for t in range(PACK):
+            nc.sync.dma_start(second_rows[t][:], vals2_v[:, t, :])
+            nc.sync.dma_start(first_rows[t][:], vals_v[:, t, :])
+
+        words_listed = held.tile([P, I], U16, name="words_listed")
+        bytes_listed = held.tile([P, I], U8, name="bytes_listed")
+        words_dealt = held.tile([P, I], U16, name="words_dealt", align_bytes=64)
+        bytes_dealt = held.tile([P, I], U8, name="bytes_dealt", align_bytes=64)
+        nc.vector.tensor_copy(words_listed[:], key_words[:].indirect(key_list[:]))
+        nc.vector.tensor_copy(bytes_listed[:], key_bytes[:].indirect(key_list[:]))
+        nc.vector.tensor_copy(dealt(words_dealt[:]), listed(words_listed[:]))
+        nc.vector.tensor_copy(dealt(bytes_dealt[:]), listed(bytes_listed[:]))
+
+        factor_bank = psum.tile([P, P], F32, name="factor_bank")
+        factors = held.tile([P, 2 * PACK], F32, name="factors")
+        nc.tensor.transpose(factor_bank[:], factor_rows[:], identity[:])
+        nc.scalar.copy(factors[:], factor_bank[:, 0 : 2 * PACK])
+        weight_scale = factors[:, 0:PACK].unsqueeze(1).to_broadcast([P, HALF, PACK])
+        value_scale = factors[:, PACK : 2 * PACK].unsqueeze(1).to_broadcast([P, P, PACK])
+
+        query_planes = held.tile([P, PACK, Q], BF16, name="query_planes")
+        query_woven = held.tile([P, Q, PACK], BF16, name="query_woven", align_bytes=64)
+        query_codes = held.tile([P, Q], U32, name="query_codes", align_bytes=64)
+        query_bytes = held.tile([P, Q], U8, name="query_bytes", align_bytes=64)
+        for t in range(PACK):
+            nc.scalar.activation(query_planes[:, t, :], user_rows[t][:].indirect(user_list[:]), COPY)
+        nc.vector.tensor_copy(
+            query_woven[:].rearrange("p (c i) t -> p c t i", i=4),
+            query_planes[:].rearrange("p t (c i) -> p c t i", i=4),
+        )
+        nc.vector.quantize_mx(
+            out=query_codes[:].bitcast(FP8X4),
+            scales=query_bytes[:],
+            in_=query_woven[:].rearrange("p q t -> p (q t)"),
+        )
+
+        weight_woven = held.tile([P, Q, PACK], BF16, name="weight_woven", align_bytes=64)
+        weight_codes = held.tile([P, Q], U32, name="weight_codes", align_bytes=64)
+        weight_bytes = held.tile([P, Q], U8, name="weight_bytes", align_bytes=64)
+        for h in range(2):
+            cols = slice(h * HALF, (h + 1) * HALF)
+            score_bank = psum.tile([P, PACK, HALF], F32, name=f"score_bank{h}")
+            for t in range(PACK):
+                slots = slice(t * P, (t + 1) * P)
+                nc.tensor.matmul_mx(
+                    out=score_bank[:, t, :],
+                    lhsT=words_dealt[:, slots].bitcast(FP4X4),
+                    lhsT_scale=bytes_dealt[:, slots],
+                    rhs=query_codes[:, cols].bitcast(FP8X4),
+                    rhs_scale=query_bytes[:, cols],
+                    start=True,
+                    stop=True,
+                )
+            nc.vector.tensor_tensor(
+                weight_woven[:, cols, :], score_bank[:].rearrange("p t q -> p q t"), weight_scale, MULT
+            )
+        nc.vector.quantize_mx(
+            out=weight_codes[:].bitcast(FP8X4),
+            scales=weight_bytes[:],
+            in_=weight_woven[:].rearrange("p q t -> p (q t)"),
+        )
+
+        result_banks = [psum.tile([P, PACK, HALF], F32, name=f"result_bank{h}") for h in range(2)]
+        result = held.tile([P, PACK, Q], F32, name="result")
+        result_woven = held.tile([P, Q, PACK], BF16, name="result_woven", align_bytes=64)
+        result_codes = held.tile([P, Q], U32, name="result_codes", align_bytes=64)
+        result_bytes = held.tile([P, Q], U8, name="result_bytes", align_bytes=64)
+        last = PACK - 1
+        for t in range(PACK):
+            first = ring.tile([P, I], F32, name="first")
+            second = ring.tile([P, I], F32, name="second")
+            larger = ring.tile([P, I], F32, name="larger")
+            nc.vector.tensor_copy(second[:], second_rows[t][:].indirect(second_list[:]))
+            if t < last:
+                nc.scalar.activation(first[:], first_rows[t][:].indirect(key_list[:]), COPY)
+                nc.vector.tensor_tensor(dealt(larger[:]), listed(first[:]), listed(second[:]), MAX)
+            else:
+                cut = SPLIT // PER_COLUMN
+                nc.vector.tensor_copy(first[:, 0:SPLIT], first_rows[t][:].indirect(key_list[:, 0:cut]))
+                nc.scalar.activation(first[:, SPLIT:I], first_rows[t][:].indirect(key_list[:, cut:]), COPY)
+                for blocks in (slice(0, SPLIT // 32), slice(SPLIT // 32, I // 32)):
+                    nc.vector.tensor_tensor(
+                        dealt(larger[:])[:, blocks], listed(first[:])[:, blocks], listed(second[:])[:, blocks], MAX
+                    )
+            turned = psum.tile([P, PACK, P], F32, name="turned", bufs=2)
+            for r in range(PACK):
+                nc.tensor.transpose(turned[:, r, :], larger[:, r * P : (r + 1) * P], identity[:])
+            value_woven = ring.tile([P, P, PACK], BF16, name="value_woven", align_bytes=64)
+            value_codes = ring.tile([P, P], U32, name="value_codes", align_bytes=64)
+            value_bytes = ring.tile([P, P], U8, name="value_bytes", align_bytes=64)
+            nc.vector.tensor_tensor(value_woven[:], turned[:].rearrange("p r e -> p e r"), value_scale, MULT)
+            nc.vector.quantize_mx(
+                out=value_codes[:].bitcast(FP8X4),
+                scales=value_bytes[:],
+                in_=value_woven[:].rearrange("p e r -> p (e r)"),
+            )
+            for h in range(2):
+                cols = slice(h * HALF, (h + 1) * HALF)
+                nc.tensor.matmul_mx(
+                    out=result_banks[h][:, t, :],
+                    lhsT=value_codes[:].bitcast(FP8X4),
+                    lhsT_scale=value_bytes[:],
+                    rhs=weight_codes[:, cols].bitcast(FP8X4),
+                    rhs_scale=weight_bytes[:, cols],
+                    start=True,
+                    stop=True,
+                )
+            if t == last:
+                nc.vector.tensor_copy(result_woven[:, 0:HALF, :], result_banks[0][:].rearrange("p t q -> p q t"))
+                nc.scalar.copy(result_woven[:, HALF:Q, :], result_banks[1][:].rearrange("p t q -> p q t"))
+            for h in (1, 0):
+                nc.scalar.copy(result[:, t, h * HALF : (h + 1) * HALF], result_banks[h][:, t, :])
+            if t == last - 1:
+                nc.sync.dma_start(out_v[:, 0:last, :], result[:, 0:last, :])
+        nc.scalar.dma_start(out_v[:, last, :], result[:, last, :])
+
+        nc.vector.quantize_mx(
+            out=result_codes[:].bitcast(FP8X4),
+            scales=result_bytes[:],
+            in_=result_woven[:].rearrange("p q t -> p (q t)"),
+        )
+        nc.sync.dma_start(out_1[0].rearrange("p q t -> p (q t)").bitcast(I32), result_codes[:].bitcast(I32))
+        for quad in range(4):
+            queue = nc.sync if quad < 2 else nc.scalar
+            queue.dma_start(
+                out_2[0, 4 * quad : 4 * quad + 4, :].bitcast(I32),
+                result_bytes[32 * quad : 32 * quad + 4, :].bitcast(I32),
+            )

@@ -52,11 +52,11 @@ def tile_attend_listedqueries_mergedvalues_lean_pl_kernel(
         factor_rows = held.tile([P, P], F32, name="factor_rows")
         identity = held.tile([P, P], F32, name="identity")
         user_rows = [held.tile([P, U], F32, name=f"user_rows{t}") for t in range(PACK)]
-        first_rows = [held.tile([P, T], F32, name=f"first_rows{t}") for t in range(PACK)]
+        first_rows = [held.tile([P, T], F32, name=f"first_rows{t}", tag=f"first_rows{t}") for t in range(PACK)]
         second_rows = [held.tile([P, X], F32, name=f"second_rows{t}") for t in range(PACK)]
 
-        nc.vector.memset(key_bytes[:].bitcast(I32), 0)
-        nc.vector.memset(factor_rows[:], 0.0)
+        nc.gpsimd.memset(factor_rows[:], 0.0)
+        nc.gpsimd.memset(key_bytes[:].bitcast(I32), 0)
         make_identity(nc, identity[:])
 
         users_v = users.rearrange("(p t) u -> p t u", t=PACK)
@@ -68,18 +68,19 @@ def tile_attend_listedqueries_mergedvalues_lean_pl_kernel(
         nc.sync.dma_start(user_rows[0][:], users_v[:, 0, :])
         nc.sync.dma_start(key_list[:], offs)
         nc.sync.dma_start(user_list[:], offs2)
-        for quad in range(4):
-            nc.scalar.dma_start(
-                key_bytes[32 * quad : 32 * quad + 4, :].bitcast(I32),
-                keys_scales[0, 4 * quad : 4 * quad + 4, :].bitcast(I32),
-            )
         for place, factor in enumerate((weight_factor, value_factor)):
-            nc.scalar.dma_start(
+            nc.sync.dma_start(
                 factor_rows[PACK * place : PACK * place + PACK, :].rearrange("t (b j) -> t b j", j=RUN),
                 factor[0].rearrange("(b t j) -> t b j", t=PACK, j=RUN),
             )
-        for t in range(1, PACK):
-            nc.sync.dma_start(user_rows[t][:], users_v[:, t, :])
+        nc.sync.dma_start(user_rows[1][:], users_v[:, 1, :])
+        nc.sync.dma_start(user_rows[2][:], users_v[:, 2, :])
+        for quad in range(4):
+            nc.sync.dma_start(
+                key_bytes[32 * quad : 32 * quad + 4, :].bitcast(I32),
+                keys_scales[0, 4 * quad : 4 * quad + 4, :].bitcast(I32),
+            )
+        nc.sync.dma_start(user_rows[3][:], users_v[:, 3, :])
         nc.sync.dma_start(second_list[:], offs3)
         for t in range(PACK):
             nc.sync.dma_start(second_rows[t][:], vals2_v[:, t, :])
@@ -122,7 +123,7 @@ def tile_attend_listedqueries_mergedvalues_lean_pl_kernel(
         weight_bytes = held.tile([P, Q], U8, name="weight_bytes", align_bytes=64)
         for h in range(2):
             cols = slice(h * HALF, (h + 1) * HALF)
-            score_bank = psum.tile([P, PACK, HALF], F32, name=f"score_bank{h}")
+            score_bank = psum.tile([P, PACK, HALF], F32, name=f"score_bank{h}", tag=f"score_bank{h}")
             for t in range(PACK):
                 slots = slice(t * P, (t + 1) * P)
                 nc.tensor.matmul_mx(
@@ -143,35 +144,34 @@ def tile_attend_listedqueries_mergedvalues_lean_pl_kernel(
             in_=weight_woven[:].rearrange("p q t -> p (q t)"),
         )
 
-        result_banks = [psum.tile([P, PACK, HALF], F32, name=f"result_bank{h}") for h in range(2)]
-        result = held.tile([P, PACK, Q], F32, name="result")
-        result_woven = held.tile([P, Q, PACK], BF16, name="result_woven", align_bytes=64)
+        last = PACK - 1
+        early_banks = [psum.tile([P, last, HALF], F32, name=f"early_bank{h}") for h in range(2)]
+        last_banks = [psum.tile([P, 1, HALF], F32, name=f"last_bank{h}", tag=f"score_bank{h}") for h in range(2)]
         result_codes = held.tile([P, Q], U32, name="result_codes", align_bytes=64)
         result_bytes = held.tile([P, Q], U8, name="result_bytes", align_bytes=64)
-        last = PACK - 1
-        for t in range(PACK):
+        cut = SPLIT // PER_COLUMN
+        turned = {}
+
+        def merge(t):
             first = ring.tile([P, I], F32, name="first")
-            second = ring.tile([P, I], F32, name="second")
+            second = held.tile([P, I], F32, name=f"second{t}", tag=f"second{t}", align_bytes=64)
             larger = ring.tile([P, I], F32, name="larger")
-            nc.vector.tensor_copy(second[:], second_rows[t][:].indirect(second_list[:]))
-            if t < last:
-                nc.scalar.activation(first[:], first_rows[t][:].indirect(key_list[:]), COPY)
-                nc.vector.tensor_tensor(dealt(larger[:]), listed(first[:]), listed(second[:]), MAX)
-            else:
-                cut = SPLIT // PER_COLUMN
-                nc.vector.tensor_copy(first[:, 0:SPLIT], first_rows[t][:].indirect(key_list[:, 0:cut]))
-                nc.scalar.activation(first[:, SPLIT:I], first_rows[t][:].indirect(key_list[:, cut:]), COPY)
-                for blocks in (slice(0, SPLIT // 32), slice(SPLIT // 32, I // 32)):
-                    nc.vector.tensor_tensor(
-                        dealt(larger[:])[:, blocks], listed(first[:])[:, blocks], listed(second[:])[:, blocks], MAX
-                    )
-            turned = psum.tile([P, PACK, P], F32, name="turned", bufs=2)
+            nc.scalar.activation(second[:], second_rows[t][:].indirect(second_list[:]), COPY)
+            nc.vector.tensor_copy(first[:, 0:SPLIT], first_rows[t][:].indirect(key_list[:, 0:cut]))
+            nc.scalar.activation(first[:, SPLIT:I], first_rows[t][:].indirect(key_list[:, cut:]), COPY)
+            for places in (slice(0, 2), slice(2, PACK)):
+                nc.vector.tensor_tensor(
+                    dealt(larger[:])[:, :, places], listed(first[:])[:, :, places], listed(second[:])[:, :, places], MAX
+                )
+            turned[t] = psum.tile([P, PACK, P], F32, name="turned", bufs=2)
             for r in range(PACK):
-                nc.tensor.transpose(turned[:, r, :], larger[:, r * P : (r + 1) * P], identity[:])
-            value_woven = ring.tile([P, P, PACK], BF16, name="value_woven", align_bytes=64)
+                nc.tensor.transpose(turned[t][:, r, :], larger[:, r * P : (r + 1) * P], identity[:])
+
+        def multiply(t):
+            value_woven = held.tile([P, P, PACK], BF16, name=f"value_woven{t}", tag=f"second{t + 1}", align_bytes=64)
             value_codes = ring.tile([P, P], U32, name="value_codes", align_bytes=64)
             value_bytes = ring.tile([P, P], U8, name="value_bytes", align_bytes=64)
-            nc.vector.tensor_tensor(value_woven[:], turned[:].rearrange("p r e -> p e r"), value_scale, MULT)
+            nc.vector.tensor_tensor(value_woven[:], turned[t][:].rearrange("p r e -> p e r"), value_scale, MULT)
             nc.vector.quantize_mx(
                 out=value_codes[:].bitcast(FP8X4),
                 scales=value_bytes[:],
@@ -180,7 +180,7 @@ def tile_attend_listedqueries_mergedvalues_lean_pl_kernel(
             for h in range(2):
                 cols = slice(h * HALF, (h + 1) * HALF)
                 nc.tensor.matmul_mx(
-                    out=result_banks[h][:, t, :],
+                    out=early_banks[h][:, t, :] if t < last else last_banks[h][:, 0, :],
                     lhsT=value_codes[:].bitcast(FP8X4),
                     lhsT_scale=value_bytes[:],
                     rhs=weight_codes[:, cols].bitcast(FP8X4),
@@ -188,14 +188,27 @@ def tile_attend_listedqueries_mergedvalues_lean_pl_kernel(
                     start=True,
                     stop=True,
                 )
-            if t == last:
-                nc.vector.tensor_copy(result_woven[:, 0:HALF, :], result_banks[0][:].rearrange("p t q -> p q t"))
-                nc.scalar.copy(result_woven[:, HALF:Q, :], result_banks[1][:].rearrange("p t q -> p q t"))
+
+        def store_rows(start, stop, sources, tag, queue):
+            rows = slice(start, stop)
+            result = held.tile([P, stop - start, Q], F32, name=f"result{start}", tag=tag)
             for h in (1, 0):
-                nc.scalar.copy(result[:, t, h * HALF : (h + 1) * HALF], result_banks[h][:, t, :])
-            if t == last - 1:
-                nc.sync.dma_start(out_v[:, 0:last, :], result[:, 0:last, :])
-        nc.scalar.dma_start(out_v[:, last, :], result[:, last, :])
+                nc.scalar.copy(result[:, :, h * HALF : (h + 1) * HALF], sources[h])
+            queue.dma_start(out_v[:, rows, :], result[:])
+
+        merge(0)
+        for t in range(1, PACK):
+            merge(t)
+            if t == PACK - 1:
+                store_rows(0, 2, [bank[:, 0:2, :] for bank in early_banks], f"first_rows{t}", nc.sync)
+            multiply(t - 1)
+        store_rows(2, 3, [bank[:, 2:3, :] for bank in early_banks], "result2", nc.sync)
+        multiply(PACK - 1)
+        result_woven = held.tile([P, Q, PACK], BF16, name="result_woven", tag=f"second{PACK}", align_bytes=64)
+        for banks, places in ((early_banks, slice(0, last)), (last_banks, slice(last, PACK))):
+            nc.vector.tensor_copy(result_woven[:, 0:HALF, places], banks[0][:].rearrange("p t q -> p q t"))
+            nc.scalar.copy(result_woven[:, HALF:Q, places], banks[1][:].rearrange("p t q -> p q t"))
+        store_rows(3, 4, [bank[:] for bank in last_banks], "result3", nc.scalar)
 
         nc.vector.quantize_mx(
             out=result_codes[:].bitcast(FP8X4),

@@ -49,74 +49,76 @@ def tile_attend_listedqueries_mergedvalues_lean_pl_kernel(
         second_list = held.tile([P, I // PER_COLUMN], U16, name="second_list")
         key_words = held.tile([P, T], U16, name="key_words")
         key_bytes = held.tile([P, T], U8, name="key_bytes")
-        factor_rows = held.tile([P, P], F32, name="factor_rows")
+        factor_rows = held.tile([2, I], F32, name="factor_rows")
+        factor_dealt = held.tile([P, I], F32, name="factor_dealt")
         identity = held.tile([P, P], F32, name="identity")
-        user_rows = [held.tile([P, U], F32, name=f"user_rows{t}") for t in range(PACK)]
+        user_rows = [held.tile([P, 2 * U], F32, name=f"user_rows{pair}") for pair in range(2)]
         first_rows = [held.tile([P, T], F32, name=f"first_rows{t}", tag=f"first_rows{t}") for t in range(PACK)]
         second_rows = [held.tile([P, X], F32, name=f"second_rows{t}") for t in range(PACK)]
 
-        nc.gpsimd.memset(factor_rows[:], 0.0)
         nc.gpsimd.memset(key_bytes[:].bitcast(I32), 0)
+        nc.gpsimd.memset(factor_dealt[:], 0.0)
         make_identity(nc, identity[:])
 
-        users_v = users.rearrange("(p t) u -> p t u", t=PACK)
+        users_v = users.rearrange("(p a t) u -> p a (t u)", a=2, t=2)
         vals_v = vals.rearrange("(p t) c -> p t c", t=PACK)
         vals2_v = vals2.rearrange("(p t) c -> p t c", t=PACK)
         out_v = out_0.rearrange("(p t) q -> p t q", t=PACK)
 
         nc.sync.dma_start(key_words[:].bitcast(I32), keys_words[0].bitcast(I32))
-        nc.sync.dma_start(user_rows[0][:], users_v[:, 0, :])
         nc.sync.dma_start(key_list[:], offs)
         nc.sync.dma_start(user_list[:], offs2)
-        for place, factor in enumerate((weight_factor, value_factor)):
-            nc.sync.dma_start(
-                factor_rows[PACK * place : PACK * place + PACK, :].rearrange("t (b j) -> t b j", j=RUN),
-                factor[0].rearrange("(b t j) -> t b j", t=PACK, j=RUN),
-            )
-        nc.sync.dma_start(user_rows[1][:], users_v[:, 1, :])
-        nc.sync.dma_start(user_rows[2][:], users_v[:, 2, :])
-        for quad in range(4):
-            nc.sync.dma_start(
-                key_bytes[32 * quad : 32 * quad + 4, :].bitcast(I32),
-                keys_scales[0, 4 * quad : 4 * quad + 4, :].bitcast(I32),
-            )
-        nc.sync.dma_start(user_rows[3][:], users_v[:, 3, :])
         nc.sync.dma_start(second_list[:], offs3)
+        nc.sync.dma_start(factor_rows[0:1, :], weight_factor)
+        nc.sync.dma_start(factor_rows[1:2, :], value_factor)
+        nc.sync.dma_start(user_rows[0][:], users_v[:, 0, :])
         for t in range(PACK):
             nc.sync.dma_start(second_rows[t][:], vals2_v[:, t, :])
+            if t == 0:
+                for r in range(4):
+                    nc.sync.dma_start(key_bytes[r:P:32, :].bitcast(I32), keys_scales[0, r:16:4, :].bitcast(I32))
+                nc.sync.dma_start(user_rows[1][:], users_v[:, 1, :])
             nc.sync.dma_start(first_rows[t][:], vals_v[:, t, :])
 
         words_listed = held.tile([P, I], U16, name="words_listed")
-        bytes_listed = held.tile([P, I], U8, name="bytes_listed")
         words_dealt = held.tile([P, I], U16, name="words_dealt", align_bytes=64)
         bytes_dealt = held.tile([P, I], U8, name="bytes_dealt", align_bytes=64)
         nc.vector.tensor_copy(words_listed[:], key_words[:].indirect(key_list[:]))
-        nc.vector.tensor_copy(bytes_listed[:], key_bytes[:].indirect(key_list[:]))
+        nc.vector.tensor_copy(dealt(bytes_dealt[:]), key_bytes[:].indirect(key_list[:]))
         nc.vector.tensor_copy(dealt(words_dealt[:]), listed(words_listed[:]))
-        nc.vector.tensor_copy(dealt(bytes_dealt[:]), listed(bytes_listed[:]))
 
-        factor_bank = psum.tile([P, P], F32, name="factor_bank")
-        factors = held.tile([P, 2 * PACK], F32, name="factors")
-        nc.tensor.transpose(factor_bank[:], factor_rows[:], identity[:])
-        nc.scalar.copy(factors[:], factor_bank[:, 0 : 2 * PACK])
-        weight_scale = factors[:, 0:PACK].unsqueeze(1).to_broadcast([P, HALF, PACK])
-        value_scale = factors[:, PACK : 2 * PACK].unsqueeze(1).to_broadcast([P, P, PACK])
+        factor_bank = psum.tile([P, PACK, P], F32, name="factor_bank")
+        factors = held.tile([P, 2, PACK], F32, name="factors")
+        nc.scalar.activation(dealt(factor_dealt[0:2, :]), listed(factor_rows[:]), COPY)
+        for t in range(PACK):
+            nc.tensor.transpose(factor_bank[:, t, :], factor_dealt[:, t * P : (t + 1) * P], identity[:])
+        nc.scalar.copy(factors[:], factor_bank[:, :, 0:2].rearrange("p t f -> p f t"))
+        weight_scale = factors[:, 0:1, :].to_broadcast([P, HALF, PACK])
+        value_scale = factors[:, 1:2, :].to_broadcast([P, P, PACK])
 
-        query_planes = held.tile([P, PACK, Q], BF16, name="query_planes")
+        query_planes = held.tile([P, PACK, Q], F32, name="query_planes")
         query_woven = held.tile([P, Q, PACK], BF16, name="query_woven", align_bytes=64)
         query_codes = held.tile([P, Q], U32, name="query_codes", align_bytes=64)
         query_bytes = held.tile([P, Q], U8, name="query_bytes", align_bytes=64)
         for t in range(PACK):
-            nc.scalar.activation(query_planes[:, t, :], user_rows[t][:].indirect(user_list[:]), COPY)
-        nc.vector.tensor_copy(
-            query_woven[:].rearrange("p (c i) t -> p c t i", i=4),
-            query_planes[:].rearrange("p t (c i) -> p c t i", i=4),
-        )
-        nc.vector.quantize_mx(
-            out=query_codes[:].bitcast(FP8X4),
-            scales=query_bytes[:],
-            in_=query_woven[:].rearrange("p q t -> p (q t)"),
-        )
+            window = user_rows[t // 2][:, (t % 2) * U : (t % 2 + 1) * U].indirect(user_list[:])
+            if t < PACK - 1:
+                nc.scalar.activation(query_planes[:, t, :], window, COPY)
+            else:
+                nc.vector.tensor_copy(query_planes[:, t, :], window)
+        for h in range(2):
+            cols = slice(h * HALF, (h + 1) * HALF)
+            nc.vector.tensor_copy(
+                query_woven[:, cols, :].rearrange("p (c i) t -> p c t i", i=4),
+                query_planes[:, :, cols].rearrange("p t (c i) -> p c t i", i=4),
+            )
+        for h in range(2):
+            cols = slice(h * HALF, (h + 1) * HALF)
+            nc.vector.quantize_mx(
+                out=query_codes[:, cols].bitcast(FP8X4),
+                scales=query_bytes[:, cols],
+                in_=query_woven[:, cols, :].rearrange("p q t -> p (q t)"),
+            )
 
         weight_woven = held.tile([P, Q, PACK], BF16, name="weight_woven", align_bytes=64)
         weight_codes = held.tile([P, Q], U32, name="weight_codes", align_bytes=64)
@@ -157,8 +159,11 @@ def tile_attend_listedqueries_mergedvalues_lean_pl_kernel(
             second = held.tile([P, I], F32, name=f"second{t}", tag=f"second{t}", align_bytes=64)
             larger = ring.tile([P, I], F32, name="larger")
             nc.scalar.activation(second[:], second_rows[t][:].indirect(second_list[:]), COPY)
-            nc.vector.tensor_copy(first[:, 0:SPLIT], first_rows[t][:].indirect(key_list[:, 0:cut]))
-            nc.scalar.activation(first[:, SPLIT:I], first_rows[t][:].indirect(key_list[:, cut:]), COPY)
+            if t == 0:
+                nc.scalar.activation(first[:], first_rows[t][:].indirect(key_list[:]), COPY)
+            else:
+                nc.vector.tensor_copy(first[:, 0:SPLIT], first_rows[t][:].indirect(key_list[:, 0:cut]))
+                nc.scalar.activation(first[:, SPLIT:I], first_rows[t][:].indirect(key_list[:, cut:]), COPY)
             for places in (slice(0, 2), slice(2, PACK)):
                 nc.vector.tensor_tensor(
                     dealt(larger[:])[:, :, places], listed(first[:])[:, :, places], listed(second[:])[:, :, places], MAX
@@ -168,9 +173,9 @@ def tile_attend_listedqueries_mergedvalues_lean_pl_kernel(
                 nc.tensor.transpose(turned[t][:, r, :], larger[:, r * P : (r + 1) * P], identity[:])
 
         def multiply(t):
-            value_woven = held.tile([P, P, PACK], BF16, name=f"value_woven{t}", tag=f"second{t + 1}", align_bytes=64)
-            value_codes = ring.tile([P, P], U32, name="value_codes", align_bytes=64)
-            value_bytes = ring.tile([P, P], U8, name="value_bytes", align_bytes=64)
+            value_woven = held.tile([P, P, PACK], BF16, name=f"value_woven{t}", tag=f"value_woven{t}" if t > 0 else "second1", align_bytes=64)
+            value_codes = held.tile([P, P], U32, name=f"value_codes{t}", tag=f"second{t + 1}" if t > 0 else "value_codes0", align_bytes=64)
+            value_bytes = held.tile([P, P], U8, name=f"value_bytes{t}", align_bytes=64)
             nc.vector.tensor_tensor(value_woven[:], turned[t][:].rearrange("p r e -> p e r"), value_scale, MULT)
             nc.vector.quantize_mx(
                 out=value_codes[:].bitcast(FP8X4),
@@ -192,7 +197,7 @@ def tile_attend_listedqueries_mergedvalues_lean_pl_kernel(
         def store_rows(start, stop, sources, tag, queue):
             rows = slice(start, stop)
             result = held.tile([P, stop - start, Q], F32, name=f"result{start}", tag=tag)
-            for h in (1, 0):
+            for h in range(2):
                 nc.scalar.copy(result[:, :, h * HALF : (h + 1) * HALF], sources[h])
             queue.dma_start(out_v[:, rows, :], result[:])
 
@@ -204,17 +209,22 @@ def tile_attend_listedqueries_mergedvalues_lean_pl_kernel(
             multiply(t - 1)
         store_rows(2, 3, [bank[:, 2:3, :] for bank in early_banks], "result2", nc.sync)
         multiply(PACK - 1)
-        result_woven = held.tile([P, Q, PACK], BF16, name="result_woven", tag=f"second{PACK}", align_bytes=64)
+        woven_halves = [
+            held.tile([P, HALF, PACK], BF16, name=f"result_woven{h}", tag=tag, align_bytes=64)
+            for h, tag in enumerate(("result_woven0", f"value_woven{last}"))
+        ]
         for banks, places in ((early_banks, slice(0, last)), (last_banks, slice(last, PACK))):
-            nc.vector.tensor_copy(result_woven[:, 0:HALF, places], banks[0][:].rearrange("p t q -> p q t"))
-            nc.scalar.copy(result_woven[:, HALF:Q, places], banks[1][:].rearrange("p t q -> p q t"))
+            nc.scalar.copy(woven_halves[0][:, :, places], banks[0][:].rearrange("p t q -> p q t"))
+            nc.vector.tensor_copy(woven_halves[1][:, :, places], banks[1][:].rearrange("p t q -> p q t"))
         store_rows(3, 4, [bank[:] for bank in last_banks], "result3", nc.scalar)
 
-        nc.vector.quantize_mx(
-            out=result_codes[:].bitcast(FP8X4),
-            scales=result_bytes[:],
-            in_=result_woven[:].rearrange("p q t -> p (q t)"),
-        )
+        for h in range(2):
+            cols = slice(h * HALF, (h + 1) * HALF)
+            nc.vector.quantize_mx(
+                out=result_codes[:, cols].bitcast(FP8X4),
+                scales=result_bytes[:, cols],
+                in_=woven_halves[h][:].rearrange("p q t -> p (q t)"),
+            )
         nc.sync.dma_start(out_1[0].rearrange("p q t -> p (q t)").bitcast(I32), result_codes[:].bitcast(I32))
         for quad in range(4):
             queue = nc.sync if quad < 2 else nc.scalar

from contextlib import ExitStack

import concourse.mybir as mybir
from concourse.masks import make_identity

D, T, I, Q, E, U, X = 512, 2048, 512, 256, 512, 1024, 1024
FLOPS = 2 * D * I * Q + 2 * I * E * Q

F32 = mybir.dt.float32
BF16 = mybir.dt.bfloat16
I32 = mybir.dt.int32
U32 = mybir.dt.uint32
U16 = mybir.dt.uint16
U8 = mybir.dt.uint8
FP8X4 = mybir.dt.float8_e4m3fn_x4
FP4X4 = mybir.dt.float4_e2m1fn_x4
COPY = mybir.ActivationFunctionType.Copy
MULT = mybir.AluOpType.mult
MAX = mybir.AluOpType.max

P = 128
PACK = 4
RUN = 8
HALF = Q // 2
PER_COLUMN = 16
SPLIT = 256


def listed(view):
    return view.rearrange("p (b t j) -> p b t j", t=PACK, j=RUN)


def dealt(view):
    return view.rearrange("p (t b j) -> p b t j", t=PACK, j=RUN)


def tile_attend_listedqueries_mergedvalues_lean_pl_kernel(
    tc, users, keys_words, keys_scales, weight_factor, vals, vals2, value_factor,
    offs, offs2, offs3, out_0, out_1, out_2,
):
    nc = tc.nc
    with ExitStack() as ctx:
        held = ctx.enter_context(tc.tile_pool(name="held", bufs=1))
        ring = ctx.enter_context(tc.tile_pool(name="ring", bufs=2))
        psum = ctx.enter_context(tc.psum_pool(name="psum", bufs=1))

        key_list = held.tile([P, I // PER_COLUMN], U16, name="key_list")
        user_list = held.tile([P, Q // PER_COLUMN], U16, name="user_list")
        second_list = held.tile([P, I // PER_COLUMN], U16, name="second_list")
        key_words = held.tile([P, T], U16, name="key_words")
        key_bytes = held.tile([P, T], U8, name="key_bytes")
        factor_rows = held.tile([2, I], F32, name="factor_rows")
        factor_dealt = held.tile([P, I], F32, name="factor_dealt")
        identity = held.tile([P, P], F32, name="identity")
        user_rows = [held.tile([P, 2 * U], F32, name=f"user_rows{pair}") for pair in range(2)]
        first_rows = [held.tile([P, T], F32, name=f"first_rows{t}", tag=f"first_rows{t}") for t in range(PACK)]
        second_rows = [held.tile([P, X], F32, name=f"second_rows{t}") for t in range(PACK)]

        nc.gpsimd.memset(key_bytes[:].bitcast(I32), 0)
        nc.gpsimd.memset(factor_dealt[:], 0.0)
        make_identity(nc, identity[:])

        users_v = users.rearrange("(p a t) u -> p a (t u)", a=2, t=2)
        vals_v = vals.rearrange("(p t) c -> p t c", t=PACK)
        vals2_v = vals2.rearrange("(p t) c -> p t c", t=PACK)
        out_v = out_0.rearrange("(p t) q -> p t q", t=PACK)

        nc.sync.dma_start(key_words[:].bitcast(I32), keys_words[0].bitcast(I32))
        nc.sync.dma_start(key_list[:], offs)
        nc.sync.dma_start(user_list[:], offs2)
        nc.sync.dma_start(second_list[:], offs3)
        nc.sync.dma_start(factor_rows[0:1, :], weight_factor)
        nc.sync.dma_start(factor_rows[1:2, :], value_factor)
        nc.sync.dma_start(user_rows[0][:], users_v[:, 0, :])
        for t in range(PACK):
            nc.sync.dma_start(second_rows[t][:], vals2_v[:, t, :])
            if t == 0:
                for r in range(4):
                    nc.sync.dma_start(key_bytes[r:P:32, :].bitcast(I32), keys_scales[0, r:16:4, :].bitcast(I32))
                nc.sync.dma_start(user_rows[1][:], users_v[:, 1, :])
            nc.sync.dma_start(first_rows[t][:], vals_v[:, t, :])

        words_listed = held.tile([P, I], U16, name="words_listed")
        words_dealt = held.tile([P, I], U16, name="words_dealt", align_bytes=64)
        bytes_dealt = held.tile([P, I], U8, name="bytes_dealt", align_bytes=64)
        nc.vector.tensor_copy(words_listed[:], key_words[:].indirect(key_list[:]))
        nc.vector.tensor_copy(dealt(bytes_dealt[:]), key_bytes[:].indirect(key_list[:]))
        nc.vector.tensor_copy(dealt(words_dealt[:]), listed(words_listed[:]))

        factor_bank = psum.tile([P, PACK, P], F32, name="factor_bank")
        factors = held.tile([P, 2, PACK], F32, name="factors")
        nc.scalar.activation(dealt(factor_dealt[0:2, :]), listed(factor_rows[:]), COPY)
        for t in range(PACK):
            nc.tensor.transpose(factor_bank[:, t, :], factor_dealt[:, t * P : (t + 1) * P], identity[:])
        nc.scalar.copy(factors[:], factor_bank[:, :, 0:2].rearrange("p t f -> p f t"))
        weight_scale = factors[:, 0:1, :].to_broadcast([P, HALF, PACK])
        value_scale = factors[:, 1:2, :].to_broadcast([P, P, PACK])

        query_planes = held.tile([P, PACK, Q], F32, name="query_planes")
        query_woven = held.tile([P, Q, PACK], BF16, name="query_woven", align_bytes=64)
        query_codes = held.tile([P, Q], U32, name="query_codes", align_bytes=64)
        query_bytes = held.tile([P, Q], U8, name="query_bytes", align_bytes=64)
        for t in range(PACK):
            window = user_rows[t // 2][:, (t % 2) * U : (t % 2 + 1) * U].indirect(user_list[:])
            if t < PACK - 1:
                nc.scalar.activation(query_planes[:, t, :], window, COPY)
            else:
                nc.vector.tensor_copy(query_planes[:, t, :], window)
        for h in range(2):
            cols = slice(h * HALF, (h + 1) * HALF)
            nc.vector.tensor_copy(
                query_woven[:, cols, :].rearrange("p (c i) t -> p c t i", i=4),
                query_planes[:, :, cols].rearrange("p t (c i) -> p c t i", i=4),
            )
        for h in range(2):
            cols = slice(h * HALF, (h + 1) * HALF)
            nc.vector.quantize_mx(
                out=query_codes[:, cols].bitcast(FP8X4),
                scales=query_bytes[:, cols],
                in_=query_woven[:, cols, :].rearrange("p q t -> p (q t)"),
            )

        weight_woven = held.tile([P, Q, PACK], BF16, name="weight_woven", align_bytes=64)
        weight_codes = held.tile([P, Q], U32, name="weight_codes", align_bytes=64)
        weight_bytes = held.tile([P, Q], U8, name="weight_bytes", align_bytes=64)
        for h in range(2):
            cols = slice(h * HALF, (h + 1) * HALF)
            score_bank = psum.tile([P, PACK, HALF], F32, name=f"score_bank{h}", tag=f"score_bank{h}")
            for t in range(PACK):
                slots = slice(t * P, (t + 1) * P)
                nc.tensor.matmul_mx(
                    out=score_bank[:, t, :],
                    lhsT=words_dealt[:, slots].bitcast(FP4X4),
                    lhsT_scale=bytes_dealt[:, slots],
                    rhs=query_codes[:, cols].bitcast(FP8X4),
                    rhs_scale=query_bytes[:, cols],
                    start=True,
                    stop=True,
                )
            nc.vector.tensor_tensor(
                weight_woven[:, cols, :], score_bank[:].rearrange("p t q -> p q t"), weight_scale, MULT
            )
        nc.vector.quantize_mx(
            out=weight_codes[:].bitcast(FP8X4),
            scales=weight_bytes[:],
            in_=weight_woven[:].rearrange("p q t -> p (q t)"),
        )

        last = PACK - 1
        early_banks = [psum.tile([P, last, HALF], F32, name=f"early_bank{h}") for h in range(2)]
        last_banks = [psum.tile([P, 1, HALF], F32, name=f"last_bank{h}", tag=f"score_bank{h}") for h in range(2)]
        result_codes = held.tile([P, Q], U32, name="result_codes", align_bytes=64)
        result_bytes = held.tile([P, Q], U8, name="result_bytes", align_bytes=64)
        cut = SPLIT // PER_COLUMN
        turned = {}

        def merge(t):
            first = ring.tile([P, I], F32, name="first")
            second = held.tile([P, I], F32, name=f"second{t}", tag=f"second{t}", align_bytes=64)
            larger = ring.tile([P, I], F32, name="larger")
            nc.scalar.activation(second[:], second_rows[t][:].indirect(second_list[:]), COPY)
            if t == 0:
                nc.scalar.activation(first[:], first_rows[t][:].indirect(key_list[:]), COPY)
            else:
                nc.vector.tensor_copy(first[:, 0:SPLIT], first_rows[t][:].indirect(key_list[:, 0:cut]))
                nc.scalar.activation(first[:, SPLIT:I], first_rows[t][:].indirect(key_list[:, cut:]), COPY)
            for places in (slice(0, 2), slice(2, PACK)):
                nc.vector.tensor_tensor(
                    dealt(larger[:])[:, :, places], listed(first[:])[:, :, places], listed(second[:])[:, :, places], MAX
                )
            turned[t] = psum.tile([P, PACK, P], F32, name="turned", bufs=2)
            for r in range(PACK):
                nc.tensor.transpose(turned[t][:, r, :], larger[:, r * P : (r + 1) * P], identity[:])

        def multiply(t):
            value_woven = held.tile([P, P, PACK], BF16, name=f"value_woven{t}", tag=f"value_woven{t}" if t > 0 else "second1", align_bytes=64)
            value_codes = held.tile([P, P], U32, name=f"value_codes{t}", tag=f"second{t + 1}" if t > 0 else "value_codes0", align_bytes=64)
            value_bytes = held.tile([P, P], U8, name=f"value_bytes{t}", align_bytes=64)
            nc.vector.tensor_tensor(value_woven[:], turned[t][:].rearrange("p r e -> p e r"), value_scale, MULT)
            nc.vector.quantize_mx(
                out=value_codes[:].bitcast(FP8X4),
                scales=value_bytes[:],
                in_=value_woven[:].rearrange("p e r -> p (e r)"),
            )
            for h in range(2):
                cols = slice(h * HALF, (h + 1) * HALF)
                nc.tensor.matmul_mx(
                    out=early_banks[h][:, t, :] if t < last else last_banks[h][:, 0, :],
                    lhsT=value_codes[:].bitcast(FP8X4),
                    lhsT_scale=value_bytes[:],
                    rhs=weight_codes[:, cols].bitcast(FP8X4),
                    rhs_scale=weight_bytes[:, cols],
                    start=True,
                    stop=True,
                )

        def store_rows(start, stop, sources, tag, queue):
            rows = slice(start, stop)
            result = held.tile([P, stop - start, Q], F32, name=f"result{start}", tag=tag)
            for h in range(2):
                nc.scalar.copy(result[:, :, h * HALF : (h + 1) * HALF], sources[h])
            queue.dma_start(out_v[:, rows, :], result[:])

        merge(0)
        for t in range(1, PACK):
            merge(t)
            if t == PACK - 1:
                store_rows(0, 2, [bank[:, 0:2, :] for bank in early_banks], f"first_rows{t}", nc.sync)
            multiply(t - 1)
        store_rows(2, 3, [bank[:, 2:3, :] for bank in early_banks], "result2", nc.sync)
        multiply(PACK - 1)
        woven_halves = [
            held.tile([P, HALF, PACK], BF16, name=f"result_woven{h}", tag=tag, align_bytes=64)
            for h, tag in enumerate(("result_woven0", f"value_woven{last}"))
        ]
        for banks, places in ((early_banks, slice(0, last)), (last_banks, slice(last, PACK))):
            nc.scalar.copy(woven_halves[0][:, :, places], banks[0][:].rearrange("p t q -> p q t"))
            nc.vector.tensor_copy(woven_halves[1][:, :, places], banks[1][:].rearrange("p t q -> p q t"))
        store_rows(3, 4, [bank[:] for bank in last_banks], "result3", nc.scalar)

        for h in range(2):
            cols = slice(h * HALF, (h + 1) * HALF)
            nc.vector.quantize_mx(
                out=result_codes[:, cols].bitcast(FP8X4),
                scales=result_bytes[:, cols],
                in_=woven_halves[h][:].rearrange("p q t -> p (q t)"),
            )
        nc.sync.dma_start(out_1[0].rearrange("p q t -> p (q t)").bitcast(I32), result_codes[:].bitcast(I32))
        for quad in range(4):
            queue = nc.sync if quad < 2 else nc.scalar
            queue.dma_start(
                out_2[0, 4 * quad : 4 * quad + 4, :].bitcast(I32),
                result_bytes[32 * quad : 32 * quad + 4, :].bitcast(I32),
            )
